import numpy as np
import ml_dtypes


def mxq(x, axis, fmt="e4m3"):
    dtype, down = {"e4m3": (ml_dtypes.float8_e4m3fn, 7), "e5m2": (ml_dtypes.float8_e5m2, 14)}[fmt]
    v = np.moveaxis(np.asarray(x, np.float32).astype(ml_dtypes.bfloat16).astype(np.float64), axis, -1)
    blocks = v.reshape(v.shape[:-1] + (-1, 32))
    amax = np.abs(blocks).max(-1, keepdims=True)
    byte = np.maximum(np.where(amax > 0, np.frexp(amax)[1] - 1 + 127, 0) - down, 1)
    scale = np.exp2(byte - 127.0)
    codes = (blocks / scale).astype(np.float32).astype(dtype).astype(np.float64)
    return np.moveaxis((codes * scale).reshape(v.shape), -1, axis)


WIDE = False


def mx_kscale(k):
    if not WIDE:
        return np.ones(k)
    levels = np.array([10, -10, 5, -5, 0])
    if k % 512:
        return np.exp2(np.random.permutation(np.resize(levels, k // 32))).repeat(32)
    a = np.empty((k // 512, 16))
    for p in range(k // 512):
        a[p, :8] = np.random.permutation(np.resize(levels, 8))
        for g in range(8):
            far = levels[np.abs(levels - a[p, g]) >= 10]
            a[p, g + 8] = far[np.random.randint(len(far))]
    return np.exp2(a.ravel()).repeat(32)


def f64(x):
    return np.asarray(x).astype(np.float64)


def striped(idx):
    return np.tile(np.asarray(idx).reshape(-1, 16).T, (8, 1)).astype(np.uint16)


def unstriped(offs):
    return offs[:16].T.reshape(-1).astype(np.int64)


E2M1 = np.array([0.0, 0.5, 1.0, 1.5, 2.0, 3.0, 4.0, 6.0, -0.0, -0.5, -1.0, -1.5, -2.0, -3.0, -4.0, -6.0])


def pack_weight(w, fmt):
    k, n = w.shape
    w = f64(np.asarray(w, np.float32).astype(ml_dtypes.bfloat16)).reshape(k // 32, 32, n)
    amax = np.abs(w).max(1)
    if fmt == "e4m3":
        byte = np.frexp(amax)[1] - 1 + 127 - 7
    else:
        mant, ex = np.frexp(amax / 6.0)
        byte = np.where(mant > 0.5, ex, ex - 1) + 127
    byte = np.clip(np.where(amax > 0, byte, 1), 1, 254)
    scaled = (w * np.exp2(127.0 - byte)[:, None, :]).reshape(k, n).astype(np.float32)
    by_word = np.ascontiguousarray(scaled.reshape(k // 512, 128, 4, n).transpose(0, 1, 3, 2))
    if fmt == "e4m3":
        words = by_word.astype(ml_dtypes.float8_e4m3fn).view(np.uint8)
    else:
        c = by_word.astype(ml_dtypes.float4_e2m1fn).view(np.uint8) & 0xF
        words = (c[..., 0::2] | (c[..., 1::2] << 4)).reshape(k // 512, 128, 2 * n)
    return np.ascontiguousarray(words), np.ascontiguousarray(byte.astype(np.uint8).reshape(k // 512, 16, n))


def unpack_weight(words, scales, fmt):
    g, _, n = scales.shape
    words = np.ascontiguousarray(words).reshape(g, 128, n, -1)
    if fmt == "e4m3":
        vals = words.view(ml_dtypes.float8_e4m3fn).astype(np.float64)
    else:
        nib = np.empty((g, 128, n, 4), np.uint8)
        nib[..., 0::2] = words & 0xF
        nib[..., 1::2] = words >> 4
        vals = E2M1[nib]
    vals = vals * np.repeat(np.exp2(scales.astype(np.float64) - 127.0), 8, axis=1)[..., None]
    return vals.transpose(0, 1, 3, 2).reshape(g * 512, n)


def sigmoid(v):
    return 1.0 / (1.0 + np.exp(-v))


D, T, U, I, J = 512, 1024, 1024, 256, 512


def setup_inputs():
    n = np.random.standard_normal
    idx = np.random.permutation(T)[:I]
    idx2 = np.random.permutation(U)[:J]
    fd = mx_kscale(D)
    fj = mx_kscale(J)
    tj = np.ones(U)
    tj[idx2] = fj
    tabbp = pack_weight(n((D, U)) / fd[:, None], "e2m1")
    return {
        "taba": (n((D, T)) * 1 / np.sqrt(D) * fd[:, None]).astype(np.float32),
        "tabb_words": tabbp[0],
        "tabb_scales": tabbp[1],
        "steep": (np.random.uniform(0.7, 2.0, (I, 1))).astype(np.float32),
        "bias": (np.random.uniform(-0.7, 0.7, (1, J))).astype(np.float32),
        "degree": (np.random.uniform(0.0, 1.0, (I, J))).astype(np.float32),
        "pw": (np.random.uniform(0.5, 3.0, (1, J))).astype(np.float32),
        "js": (np.random.uniform(0.5, 2.0, (1, J)) * fj).astype(np.float32),
        "brows": (n((D, U)) / tj).astype(np.float32),
        "old": (n((D, T)) * 2.0).astype(np.float32),
        "fade": (np.random.uniform(0.5, 1.0, (1, T))).astype(np.float32),
        "offs": striped(idx),
        "offs2": striped(idx2),
    }


def reference(taba, tabb_words, tabb_scales, steep, bias, degree, pw, js, brows, old, fade, offs, offs2):
    idx = unstriped(offs)
    idx2 = unstriped(offs2)
    tabbu = unpack_weight(tabb_words, tabb_scales, "e2m1")
    tabaidxq = mxq(f64(taba)[:, idx], 0, "e4m3")
    tabbidx2g = tabbu[:, idx2]
    s = tabaidxq.T @ tabbidx2g
    mg = sigmoid(s * f64(steep) + f64(bias))
    dmg = f64(pw) * (mg - f64(degree)) * 2.0
    ds = dmg * mg * (1.0 - mg) * f64(steep)
    gs = ds * f64(js)
    gt1 = gs.T
    bt = f64(brows)[:, idx2].T
    btq = mxq(bt, 0, "e4m3")
    gt1q = mxq(gt1, 0, "e4m3")
    gx1 = btq.T @ gt1q
    gf = np.zeros((D, T))
    gf[:, idx] = gx1
    y = f64(old) * f64(fade) + gf
    return y

@@ -1,0 +1,209 @@
+from contextlib import ExitStack
+
+import concourse.mybir as mybir
+from concourse.masks import make_identity
+
+D, T, U, I, J = 512, 1024, 1024, 256, 512
+FLOPS = 2 * D * I * J * 2
+
+F32 = mybir.dt.float32
+BF16 = mybir.dt.bfloat16
+I32 = mybir.dt.int32
+U32 = mybir.dt.uint32
+U16 = mybir.dt.uint16
+U8 = mybir.dt.uint8
+FP8X4 = mybir.dt.float8_e4m3fn_x4
+FP4X4 = mybir.dt.float4_e2m1fn_x4
+ALU = mybir.AluOpType
+ACT = mybir.ActivationFunctionType
+
+P = 128
+BANK = 512
+SCALAR_TILES = (1, 3)
+ROW_BIAS, ROW_STEEP, ROWS = 0, 4, 8
+ROW_PW, ROW_JS, ROW_FADE, LATE_ROWS = 0, 4, 8, 16
+
+
+def tile_attend_bpairfit_x_kernel(tc, taba, tabb_words, tabb_scales, steep, bias, degree, pw, js, brows, old, fade,
+                                   offs, offs2, out):
+    nc = tc.nc
+    with ExitStack() as ctx:
+        sb = ctx.enter_context(tc.tile_pool(name="sb", bufs=1))
+        ps = ctx.enter_context(tc.psum_pool(name="ps", bufs=1))
+
+        def bank(n):
+            return ps.tile([P, BANK], F32, name="bank%d" % n, tag="bank%d" % n)
+
+        def sbuf(name, shape, dtype):
+            return sb.tile(shape, dtype, name=name, align_bytes=64)
+
+        list_i = sb.tile([P, I // 16], U16, name="list_i")
+        list_j = sb.tile([P, J // 16], U16, name="list_j")
+        words = sbuf("words", [P, U], U16)
+        scales = sbuf("scales", [P, U], U8)
+        rows = sbuf("rows", [P, P], F32)
+        ident = sbuf("ident", [P, P], F32)
+        warm = sbuf("warm", [P, 1], F32)
+        a_raw = [sbuf("a_raw%d" % g, [P, 2, T], F32) for g in range(2)]
+        b_raw = [sbuf("b_raw%d" % k, [P, U], F32) for k in range(4)]
+        old_raw = [sbuf("old_raw%d" % g, [P, 4, BANK], F32) for g in range(2)]
+        deg = sbuf("deg", [P, 2, J], F32)
+        gf = [sbuf("gf%d" % k, [P, T], F32) for k in range(4)]
+
+        late_rows = sbuf("late_rows", [P, P], F32)
+        nc.gpsimd.memset(scales[:].bitcast(I32), 0)
+        nc.gpsimd.memset(rows[:], 0.0)
+        nc.gpsimd.memset(late_rows[:], 0.0)
+        make_identity(nc, ident[:])
+
+        taba_v = taba.rearrange("(p t) c -> p t c", t=4)
+        nc.sync.dma_start(list_j[:], offs2)
+        nc.sync.dma_start(words[:].bitcast(I32), tabb_words[0].bitcast(I32))
+        nc.sync.dma_start(list_i[:], offs)
+        nc.sync.dma_start(a_raw[0][:], taba_v[:, 0:2, :])
+        nc.sync.dma_start(a_raw[1][:], taba_v[:, 2:4, :])
+        for q in range(4):
+            nc.scalar.dma_start(scales[32 * q : 32 * q + 4, :].bitcast(I32), tabb_scales[0, 4 * q : 4 * q + 4, :].bitcast(I32))
+        nc.scalar.dma_start(rows[ROW_BIAS : ROW_BIAS + 4, :], bias.rearrange("o (r c) -> (o r) c", c=P))
+        nc.scalar.dma_start(rows[ROW_STEEP : ROW_STEEP + 2, :], steep.rearrange("(r c) o -> r (c o)", c=P))
+        nc.scalar.activation(warm[:], ident[:, 0:1], ACT.Sigmoid)
+        nc.sync.dma_start(b_raw[0][:], brows[0:P, :])
+        for first, vec in ((ROW_PW, pw), (ROW_JS, js), (ROW_FADE, fade)):
+            n = vec.shape[1] // P
+            nc.sync.dma_start(late_rows[first : first + n, :], vec.rearrange("o (r c) -> (o r) c", c=P))
+        nc.sync.dma_start(deg[:], degree.rearrange("(h p) j -> p h j", p=P))
+        for k in range(1, 4):
+            nc.sync.dma_start(b_raw[k][:], brows[P * k : P * (k + 1), :])
+        old_v = old.rearrange("(k p) t -> p k t", p=P)
+        for g in range(2):
+            nc.sync.dma_start(old_raw[g][:], old_v[:, :, BANK * g : BANK * (g + 1)])
+
+        for k in range(4):
+            nc.vector.memset(gf[k][:], 0.0)
+
+        cols_ps = bank(0)
+        nc.tensor.transpose(cols_ps[:, 0:P], rows[:], ident[:])
+        cols = sbuf("cols", [P, ROWS], F32)
+        nc.scalar.copy(cols[:], cols_ps[:, 0:ROWS])
+
+        b_words = sbuf("b_words", [P, J], U16)
+        b_scales = sbuf("b_scales", [P, J], U8)
+        nc.vector.tensor_copy(b_words[:], words[:].indirect(list_j[:]))
+        nc.vector.tensor_copy(b_scales[:], scales[:].indirect(list_j[:]))
+
+        bias_ps = bank(1)
+        for r in range(4):
+            nc.tensor.transpose(bias_ps[:, P * r : P * (r + 1)], cols[:, ROW_BIAS + r : ROW_BIAS + r + 1].to_broadcast([P, P]), ident[:])
+        bias_b = sbuf("bias_b", [P, J], F32)
+        nc.scalar.copy(bias_b[:], bias_ps[:])
+
+        a_in = sbuf("a_in", [P, I, 4], BF16)
+        for t in range(4):
+            nc.vector.tensor_copy(a_in[:, :, t], a_raw[t // 2][:, t % 2, :].indirect(list_i[:]))
+        a_codes = sbuf("a_codes", [P, I], U32)
+        a_scales = sbuf("a_scales", [P, I], U8)
+        nc.vector.quantize_mx(out=a_codes[:].bitcast(FP8X4), scales=a_scales[:], in_=a_in[:].rearrange("p i t -> p (i t)"))
+
+        s_ps = [bank(3), bank(4)]
+        for h in range(2):
+            nc.tensor.matmul_mx(out=s_ps[h][:], lhsT=a_codes[:, P * h : P * (h + 1)].bitcast(FP8X4), lhsT_scale=a_scales[:, P * h : P * (h + 1)],
+                                rhs=b_words[:].bitcast(FP4X4), rhs_scale=b_scales[:], start=True, stop=True)
+
+        late_ps = bank(7)
+        nc.tensor.transpose(late_ps[:, 0:P], late_rows[:], ident[:])
+        late_cols = sbuf("late_cols", [P, LATE_ROWS], F32)
+        nc.scalar.copy(late_cols[:], late_ps[:, 0:LATE_ROWS])
+        w_col = sbuf("w_col", [P, 4], F32)
+        nc.vector.scalar_tensor_tensor(w_col[:], late_cols[:, ROW_PW : ROW_PW + 4], -2.0, late_cols[:, ROW_JS : ROW_JS + 4], ALU.mult, ALU.mult)
+        w_ps = bank(2)
+        for r in range(4):
+            nc.tensor.transpose(w_ps[:, P * r : P * (r + 1)], w_col[:, r : r + 1].to_broadcast([P, P]), ident[:])
+
+        bt_in = [sbuf("bt_in%d" % k, [P, P, 4], BF16) for k in range(4)]
+        bt_codes = [sbuf("bt_codes%d" % k, [P, P], U32) for k in range(4)]
+        bt_scales = [sbuf("bt_scales%d" % k, [P, P], U8) for k in range(4)]
+
+        def gather_b(k):
+            picked = sbuf("b_picked%d" % k, [P, J], BF16)
+            if k in SCALAR_TILES:
+                cast = sbuf("b_cast%d" % k, [P, U], BF16)
+                nc.scalar.activation(cast[:], b_raw[k][:], ACT.Copy)
+                nc.scalar.activation(picked[:], cast[:].indirect(list_j[:]), ACT.Copy)
+            else:
+                nc.vector.tensor_copy(picked[:], b_raw[k][:].indirect(list_j[:]))
+            pairs = picked[:].bitcast(F32)
+            turned = bank(k % 2)
+            for u in range(2):
+                nc.tensor.transpose(turned[:, P * u : P * (u + 1)], pairs[:, u : 2 * P : 2], ident[:])
+            nc.scalar.copy(bt_in[k][:].rearrange("p d t -> p (d t)").bitcast(F32).rearrange("p (d u) -> p d u", u=2),
+                           turned[:, 0 : 2 * P].rearrange("p (u d) -> p d u", u=2))
+
+        def quantize_b(k):
+            nc.vector.quantize_mx(out=bt_codes[k][:].bitcast(FP8X4), scales=bt_scales[k][:], in_=bt_in[k][:].rearrange("p d t -> p (d t)"))
+
+        z = [sbuf("z%d" % h, [P, J], F32) for h in range(2)]
+        mg = [sbuf("mg%d" % h, [P, J], F32) for h in range(2)]
+        miss = [sbuf("miss%d" % h, [P, J], F32) for h in range(2)]
+        slope = [sbuf("slope%d" % h, [P, J], F32) for h in range(2)]
+        ds = [sbuf("ds%d" % h, [P, J], F32) for h in range(2)]
+        gs = [sbuf("gs%d" % h, [P, J], BF16) for h in range(2)]
+        steep_col = [cols[:, ROW_STEEP + h : ROW_STEEP + h + 1] for h in range(2)]
+        for h in range(2):
+            nc.vector.scalar_tensor_tensor(z[h][:], s_ps[h][:], steep_col[h], bias_b[:], ALU.mult, ALU.add)
+            nc.scalar.activation(mg[h][:], z[h][:], ACT.Sigmoid)
+        gather_b(0)
+        for h in range(2):
+            nc.vector.scalar_tensor_tensor(slope[h][:], mg[h][:], 1.0, mg[h][:], ALU.subtract, ALU.mult)
+            nc.vector.tensor_tensor(miss[h][:], mg[h][:], deg[:, h, :], ALU.subtract)
+        gather_b(1)
+        for h in range(2):
+            nc.vector.scalar_tensor_tensor(ds[h][:], miss[h][:], steep_col[h], slope[h][:], ALU.mult, ALU.mult)
+        g_in = sbuf("g_in", [P, I, 4], BF16)
+        g_in_pairs = g_in[:].rearrange("p i t -> p (i t)").bitcast(F32).rearrange("p (i u) -> p i u", u=2)
+        for h in range(2):
+            nc.vector.tensor_tensor(gs[h][:], w_ps[:], ds[h][:], ALU.mult)
+            pairs = gs[h][:].bitcast(F32)
+            turned = bank(3 + h)
+            for u in range(2):
+                nc.tensor.transpose(turned[:, P * u : P * (u + 1)], pairs[:, u : 2 * P : 2], ident[:])
+            nc.scalar.copy(g_in_pairs[:, P * h : P * (h + 1), :], turned[:, 0 : 2 * P].rearrange("p (u i) -> p i u", u=2))
+        quantize_b(0)
+        gather_b(2)
+        g_codes = sbuf("g_codes", [P, I], U32)
+        g_scales = sbuf("g_scales", [P, I], U8)
+        nc.vector.quantize_mx(out=g_codes[:].bitcast(FP8X4), scales=g_scales[:], in_=g_in[:].rearrange("p i t -> p (i t)"))
+        quantize_b(1)
+        gather_b(3)
+
+        gx = [sbuf("gx%d" % k, [P, I], F32) for k in range(4)]
+
+        def product(k):
+            gx_ps = bank((7, 2)[k % 2])
+            nc.tensor.matmul_mx(out=gx_ps[:, 0:I], lhsT=bt_codes[k][:].bitcast(FP8X4), lhsT_scale=bt_scales[k][:],
+                                rhs=g_codes[:].bitcast(FP8X4), rhs_scale=g_scales[:], start=True, stop=True)
+            nc.scalar.copy(gx[k][:], gx_ps[:, 0:I])
+
+        product(0)
+        product(1)
+        quantize_b(2)
+        quantize_b(3)
+        product(2)
+        product(3)
+
+        faded_t = [sbuf("faded_t%d" % c, [P, D], F32) for c in range(8)]
+        for c in range(8):
+            turned = bank(5 + c % 2)
+            for k in range(4):
+                nc.tensor.transpose(turned[:, P * k : P * (k + 1)], old_raw[c // 4][:, k, P * (c % 4) : P * (c % 4 + 1)], ident[:])
+            nc.scalar.activation(faded_t[c][:], turned[:], ACT.Copy, scale=late_cols[:, ROW_FADE + c : ROW_FADE + c + 1])
+
+        back_banks = ((3, 4), (5, 6), (0, 1), (3, 4))
+        for k in range(4):
+            nc.vector.tensor_copy(gf[k][:].indirect(list_i[:]), gx[k][:])
+            for g in range(2):
+                faded = bank(back_banks[k][g])
+                for c in range(4):
+                    nc.tensor.transpose(faded[:, P * c : P * (c + 1)], faded_t[4 * g + c][:, P * k : P * (k + 1)], ident[:])
+                res = sbuf("res%d_%d" % (k, g), [P, BANK], F32)
+                nc.vector.tensor_tensor(res[:], faded[:], gf[k][:, BANK * g : BANK * (g + 1)], ALU.add)
+                nc.sync.dma_start(out[P * k : P * (k + 1), BANK * g : BANK * (g + 1)], res[:])

@@ -4,7 +4,7 @@ import concourse.mybir as mybir
 from concourse.masks import make_identity
 
 D, T, U, I, J = 512, 1024, 1024, 256, 512
-FLOPS = 2 * D * I * J * 2
+FLOPS = 2 * (2 * D * I * J)
 
 F32 = mybir.dt.float32
 BF16 = mybir.dt.bfloat16
@@ -18,10 +18,14 @@ ALU = mybir.AluOpType
 ACT = mybir.ActivationFunctionType
 
 P = 128
+PACK = 4
 BANK = 512
-SCALAR_TILES = (1, 3)
-ROW_BIAS, ROW_STEEP, ROWS = 0, 4, 8
-ROW_PW, ROW_JS, ROW_FADE, LATE_ROWS = 0, 4, 8, 16
+D_TILES = D // P
+I_TILES = I // P
+T_HALVES = T // BANK
+T_CHUNKS = T // P
+POOL_TILES = 2
+SCALAR_TILE = 1
 
 
 def tile_attend_bpairfit_x_kernel(tc, taba, tabb_words, tabb_scales, steep, bias, degree, pw, js, brows, old, fade,
@@ -34,176 +38,225 @@ def tile_attend_bpairfit_x_kernel(tc, taba, tabb_words, tabb_scales, steep, bias
         def bank(n):
             return ps.tile([P, BANK], F32, name="bank%d" % n, tag="bank%d" % n)
 
-        def sbuf(name, shape, dtype):
-            return sb.tile(shape, dtype, name=name, align_bytes=64)
+        def sbuf(name, shape, dtype, after=None):
+            return sb.tile(shape, dtype, name=name, tag=after or name, align_bytes=64)
+
+        def rows_of(x, k):
+            return x[P * k : P * (k + 1), :]
+
+        def block(x, c, width=P):
+            return x[:, width * c : width * (c + 1)]
+
+        def quantise(codes, scale_bytes, grouped):
+            nc.vector.quantize_mx(out=codes.bitcast(FP8X4), scales=scale_bytes, in_=grouped.rearrange("p c t -> p (c t)"))
+
+        def spread(target, column, c):
+            nc.tensor.transpose(block(target, c), column.to_broadcast([P, P]), ident[:])
+
+        def turn_pairs(values, target):
+            pairs = values.bitcast(F32)
+            for u in range(2):
+                nc.tensor.transpose(block(target, u), pairs[:, u : 2 * P : 2], ident[:])
+
+        def group_pairs(grouped, turned):
+            nc.scalar.copy(grouped.rearrange("p c t -> p (c t)").bitcast(F32).rearrange("p (c u) -> p c u", u=2),
+                           turned[:, 0 : 2 * P].rearrange("p (u c) -> p c u", u=2))
 
         list_i = sb.tile([P, I // 16], U16, name="list_i")
         list_j = sb.tile([P, J // 16], U16, name="list_j")
         words = sbuf("words", [P, U], U16)
         scales = sbuf("scales", [P, U], U8)
-        rows = sbuf("rows", [P, P], F32)
+        fade_rows = sbuf("fade_rows", [P, P], F32)
         ident = sbuf("ident", [P, P], F32)
         warm = sbuf("warm", [P, 1], F32)
-        a_raw = [sbuf("a_raw%d" % g, [P, 2, T], F32) for g in range(2)]
-        b_raw = [sbuf("b_raw%d" % k, [P, U], F32) for k in range(4)]
-        old_raw = [sbuf("old_raw%d" % g, [P, 4, BANK], F32) for g in range(2)]
-        deg = sbuf("deg", [P, 2, J], F32)
-        gf = [sbuf("gf%d" % k, [P, T], F32) for k in range(4)]
+        a_plane = [sbuf("a_plane%d" % t, [P, T], F32) for t in range(PACK)]
+        b_raw = [sbuf("b_raw%d" % k, [P, U], F32) for k in range(D_TILES)]
+        old_rows = [sbuf("old_rows%d" % k, [P, T], F32) for k in range(POOL_TILES)]
+        old_half = [sbuf("old_half%d" % g, [P, D_TILES - POOL_TILES, BANK], F32) for g in range(T_HALVES)]
+        deg = sbuf("deg", [P, I_TILES, J], F32)
+        bias_col, pw_col, js_col = [sbuf(name, [P, PACK], F32) for name in ("bias_col", "pw_col", "js_col")]
+        steep_col = sbuf("steep_col", [P, I_TILES], F32)
+        gf = [sbuf("gf%d" % k, [P, T], F32) for k in range(D_TILES)]
 
-        late_rows = sbuf("late_rows", [P, P], F32)
         nc.gpsimd.memset(scales[:].bitcast(I32), 0)
-        nc.gpsimd.memset(rows[:], 0.0)
-        nc.gpsimd.memset(late_rows[:], 0.0)
+        nc.gpsimd.memset(fade_rows[:], 0.0)
         make_identity(nc, ident[:])
+        nc.scalar.activation(warm[:], ident[:, 0:1], ACT.Sigmoid)
+        for k in range(D_TILES):
+            (nc.vector, nc.gpsimd)[k // 2].memset(gf[k][:].bitcast(I32), 0)
 
-        taba_v = taba.rearrange("(p t) c -> p t c", t=4)
+        def load_scales(q):
+            nc.sync.dma_start(scales[32 * q : 32 * q + 4, :].bitcast(I32), tabb_scales[0, 4 * q : 4 * q + 4, :].bitcast(I32))
+
+        taba_planes = taba.rearrange("(p t) c -> p t c", t=PACK)
+        nc.sync.dma_start(list_i[:], offs)
+        nc.sync.dma_start(a_plane[0][:], taba_planes[:, 0, :])
         nc.sync.dma_start(list_j[:], offs2)
         nc.sync.dma_start(words[:].bitcast(I32), tabb_words[0].bitcast(I32))
-        nc.sync.dma_start(list_i[:], offs)
-        nc.sync.dma_start(a_raw[0][:], taba_v[:, 0:2, :])
-        nc.sync.dma_start(a_raw[1][:], taba_v[:, 2:4, :])
-        for q in range(4):
-            nc.scalar.dma_start(scales[32 * q : 32 * q + 4, :].bitcast(I32), tabb_scales[0, 4 * q : 4 * q + 4, :].bitcast(I32))
-        nc.scalar.dma_start(rows[ROW_BIAS : ROW_BIAS + 4, :], bias.rearrange("o (r c) -> (o r) c", c=P))
-        nc.scalar.dma_start(rows[ROW_STEEP : ROW_STEEP + 2, :], steep.rearrange("(r c) o -> r (c o)", c=P))
-        nc.scalar.activation(warm[:], ident[:, 0:1], ACT.Sigmoid)
-        nc.sync.dma_start(b_raw[0][:], brows[0:P, :])
-        for first, vec in ((ROW_PW, pw), (ROW_JS, js), (ROW_FADE, fade)):
-            n = vec.shape[1] // P
-            nc.sync.dma_start(late_rows[first : first + n, :], vec.rearrange("o (r c) -> (o r) c", c=P))
+        for q in range(3):
+            load_scales(q)
+        nc.sync.dma_start(a_plane[1][:], taba_planes[:, 1, :])
+        load_scales(3)
+        for t in (2, 3):
+            nc.sync.dma_start(a_plane[t][:], taba_planes[:, t, :])
+        nc.sync.dma_start(bias_col[:], bias.rearrange("o (p r) -> (o p) r", r=PACK))
+        with nc.allow_non_contiguous_dma(reason="one steepness to a partition"):
+            nc.sync.dma_start(steep_col[:], steep.rearrange("(h p) o -> p (h o)", p=P))
+        for k in (0, 1):
+            nc.sync.dma_start(b_raw[k][:], rows_of(brows, k))
+        nc.sync.dma_start(pw_col[:], pw.rearrange("o (p r) -> (o p) r", r=PACK))
+        nc.sync.dma_start(js_col[:], js.rearrange("o (p r) -> (o p) r", r=PACK))
+        nc.sync.dma_start(fade_rows[0:T_CHUNKS, :], fade.rearrange("o (c p) -> (o c) p", p=P))
+        nc.sync.dma_start(b_raw[2][:], rows_of(brows, 2))
         nc.sync.dma_start(deg[:], degree.rearrange("(h p) j -> p h j", p=P))
-        for k in range(1, 4):
-            nc.sync.dma_start(b_raw[k][:], brows[P * k : P * (k + 1), :])
-        old_v = old.rearrange("(k p) t -> p k t", p=P)
-        for g in range(2):
-            nc.sync.dma_start(old_raw[g][:], old_v[:, :, BANK * g : BANK * (g + 1)])
-
-        for k in range(4):
-            nc.vector.memset(gf[k][:], 0.0)
-
-        cols_ps = bank(0)
-        nc.tensor.transpose(cols_ps[:, 0:P], rows[:], ident[:])
-        cols = sbuf("cols", [P, ROWS], F32)
-        nc.scalar.copy(cols[:], cols_ps[:, 0:ROWS])
-
-        b_words = sbuf("b_words", [P, J], U16)
-        b_scales = sbuf("b_scales", [P, J], U8)
-        nc.vector.tensor_copy(b_words[:], words[:].indirect(list_j[:]))
-        nc.vector.tensor_copy(b_scales[:], scales[:].indirect(list_j[:]))
+        nc.sync.dma_start(b_raw[3][:], rows_of(brows, 3))
+        for k in range(POOL_TILES):
+            nc.sync.dma_start(old_rows[k][:], rows_of(old, k))
+        old_rest = old[P * POOL_TILES :, :].rearrange("(k p) t -> p k t", p=P)
+        for g in range(T_HALVES):
+            nc.sync.dma_start(old_half[g][:], old_rest[:, :, BANK * g : BANK * (g + 1)])
 
         bias_ps = bank(1)
-        for r in range(4):
-            nc.tensor.transpose(bias_ps[:, P * r : P * (r + 1)], cols[:, ROW_BIAS + r : ROW_BIAS + r + 1].to_broadcast([P, P]), ident[:])
-        bias_b = sbuf("bias_b", [P, J], F32)
-        nc.scalar.copy(bias_b[:], bias_ps[:])
+        for r in range(PACK):
+            spread(bias_ps, bias_col[:, r : r + 1], r)
+        bias_all = sbuf("bias_all", [P, J], F32)
+        nc.scalar.copy(bias_all[:].rearrange("p (c r) -> p c r", r=PACK), bias_ps[:].rearrange("p (r c) -> p c r", r=PACK))
 
-        a_in = sbuf("a_in", [P, I, 4], BF16)
-        for t in range(4):
-            nc.vector.tensor_copy(a_in[:, :, t], a_raw[t // 2][:, t % 2, :].indirect(list_i[:]))
+        a_picked = sbuf("a_picked", [P, PACK, I], F32)
+        b_words = sbuf("b_words", [P, J], U16)
+        b_scales = sbuf("b_scales", [P, J], U8)
+        nc.vector.tensor_copy(a_picked[:, 0, :], a_plane[0][:].indirect(list_i[:]))
+        nc.vector.tensor_copy(b_words[:], words[:].indirect(list_j[:]))
+        nc.vector.tensor_copy(b_scales[:], scales[:].indirect(list_j[:]))
+        for t in range(1, PACK):
+            nc.vector.tensor_copy(a_picked[:, t, :], a_plane[t][:].indirect(list_i[:]))
+        a_grouped = sbuf("a_grouped", [P, I, PACK], BF16)
+        nc.vector.tensor_copy(a_grouped[:].rearrange("p (c i) t -> p c t i", i=4), a_picked[:].rearrange("p t (c i) -> p c t i", i=4))
         a_codes = sbuf("a_codes", [P, I], U32)
         a_scales = sbuf("a_scales", [P, I], U8)
-        nc.vector.quantize_mx(out=a_codes[:].bitcast(FP8X4), scales=a_scales[:], in_=a_in[:].rearrange("p i t -> p (i t)"))
-
-        s_ps = [bank(3), bank(4)]
-        for h in range(2):
-            nc.tensor.matmul_mx(out=s_ps[h][:], lhsT=a_codes[:, P * h : P * (h + 1)].bitcast(FP8X4), lhsT_scale=a_scales[:, P * h : P * (h + 1)],
+        quantise(a_codes[:], a_scales[:], a_grouped[:])
+        s_ps = [bank(3 + h) for h in range(I_TILES)]
+        for h in range(I_TILES):
+            nc.tensor.matmul_mx(out=s_ps[h][:], lhsT=block(a_codes, h).bitcast(FP8X4), lhsT_scale=block(a_scales, h),
                                 rhs=b_words[:].bitcast(FP4X4), rhs_scale=b_scales[:], start=True, stop=True)
 
-        late_ps = bank(7)
-        nc.tensor.transpose(late_ps[:, 0:P], late_rows[:], ident[:])
-        late_cols = sbuf("late_cols", [P, LATE_ROWS], F32)
-        nc.scalar.copy(late_cols[:], late_ps[:, 0:LATE_ROWS])
-        w_col = sbuf("w_col", [P, 4], F32)
-        nc.vector.scalar_tensor_tensor(w_col[:], late_cols[:, ROW_PW : ROW_PW + 4], -2.0, late_cols[:, ROW_JS : ROW_JS + 4], ALU.mult, ALU.mult)
+        w_col = sbuf("w_col", [P, PACK], F32)
+        nc.gpsimd.tensor_tensor(w_col[:], pw_col[:], js_col[:], ALU.mult)
         w_ps = bank(2)
-        for r in range(4):
-            nc.tensor.transpose(w_ps[:, P * r : P * (r + 1)], w_col[:, r : r + 1].to_broadcast([P, P]), ident[:])
+        for r in range(PACK):
+            spread(w_ps, w_col[:, r : r + 1], r)
+        fade_ps = bank(7)
+        nc.tensor.transpose(block(fade_ps, 0), fade_rows[:], ident[:])
+        fade_col = sbuf("fade_col", [P, T_CHUNKS], F32)
+        nc.scalar.copy(fade_col[:], fade_ps[:, 0:T_CHUNKS])
 
-        bt_in = [sbuf("bt_in%d" % k, [P, P, 4], BF16) for k in range(4)]
-        bt_codes = [sbuf("bt_codes%d" % k, [P, P], U32) for k in range(4)]
-        bt_scales = [sbuf("bt_scales%d" % k, [P, P], U8) for k in range(4)]
+        b_picked, bt_grouped, bt_codes, bt_scales, fade_all = {}, {}, {}, {}, {}
 
-        def gather_b(k):
-            picked = sbuf("b_picked%d" % k, [P, J], BF16)
-            if k in SCALAR_TILES:
-                cast = sbuf("b_cast%d" % k, [P, U], BF16)
-                nc.scalar.activation(cast[:], b_raw[k][:], ACT.Copy)
-                nc.scalar.activation(picked[:], cast[:].indirect(list_j[:]), ACT.Copy)
+        def gather_b(k, window, after=None):
+            b_picked[k] = sbuf("b_picked%d" % k, [P, J], BF16, after)
+            if k == SCALAR_TILE:
+                nc.scalar.activation(b_picked[k][:], window[:].indirect(list_j[:]), ACT.Copy)
             else:
-                nc.vector.tensor_copy(picked[:], b_raw[k][:].indirect(list_j[:]))
-            pairs = picked[:].bitcast(F32)
+                nc.vector.tensor_copy(b_picked[k][:], window[:].indirect(list_j[:]))
+
+        def turn_b(k, after=None):
             turned = bank(k % 2)
-            for u in range(2):
-                nc.tensor.transpose(turned[:, P * u : P * (u + 1)], pairs[:, u : 2 * P : 2], ident[:])
-            nc.scalar.copy(bt_in[k][:].rearrange("p d t -> p (d t)").bitcast(F32).rearrange("p (d u) -> p d u", u=2),
-                           turned[:, 0 : 2 * P].rearrange("p (u d) -> p d u", u=2))
+            turn_pairs(b_picked[k][:], turned)
+            bt_grouped[k] = sbuf("bt_grouped%d" % k, [P, P, PACK], BF16, after)
+            group_pairs(bt_grouped[k][:], turned)
 
-        def quantize_b(k):
-            nc.vector.quantize_mx(out=bt_codes[k][:].bitcast(FP8X4), scales=bt_scales[k][:], in_=bt_in[k][:].rearrange("p d t -> p (d t)"))
+        def quantise_b(k, after=None):
+            bt_codes[k] = sbuf("bt_codes%d" % k, [P, P], U32, after)
+            bt_scales[k] = sbuf("bt_scales%d" % k, [P, P], U8)
+            quantise(bt_codes[k][:], bt_scales[k][:], bt_grouped[k][:])
 
-        z = [sbuf("z%d" % h, [P, J], F32) for h in range(2)]
-        mg = [sbuf("mg%d" % h, [P, J], F32) for h in range(2)]
-        miss = [sbuf("miss%d" % h, [P, J], F32) for h in range(2)]
-        slope = [sbuf("slope%d" % h, [P, J], F32) for h in range(2)]
-        ds = [sbuf("ds%d" % h, [P, J], F32) for h in range(2)]
-        gs = [sbuf("gs%d" % h, [P, J], BF16) for h in range(2)]
-        steep_col = [cols[:, ROW_STEEP + h : ROW_STEEP + h + 1] for h in range(2)]
-        for h in range(2):
-            nc.vector.scalar_tensor_tensor(z[h][:], s_ps[h][:], steep_col[h], bias_b[:], ALU.mult, ALU.add)
+        def spread_fade(g, after):
+            spread_ps = bank(5 + g)
+            for c in range(BANK // P):
+                chunk = g * (BANK // P) + c
+                spread(spread_ps, fade_col[:, chunk : chunk + 1], c)
+            fade_all[g] = sbuf("fade_all%d" % g, [P, BANK], F32, after)
+            nc.scalar.copy(fade_all[g][:], spread_ps[:])
+
+        b_cast = sbuf("b_cast", [P, U], BF16)
+        nc.scalar.activation(b_cast[:], b_raw[SCALAR_TILE][:], ACT.Copy)
+        gather_b(0, b_raw[0], "a_picked")
+
+        z = [sbuf("z0", [P, J], F32, "b_raw0"), sbuf("z1", [P, J], F32)]
+        mg, slope, miss, ds = [[sbuf("%s%d" % (name, h), [P, J], F32) for h in range(I_TILES)] for name in ("mg", "slope", "miss", "ds")]
+        gs = [sbuf("gs%d" % h, [P, J], BF16) for h in range(I_TILES)]
+        for h in range(I_TILES):
+            nc.vector.scalar_tensor_tensor(z[h][:], s_ps[h][:], steep_col[:, h : h + 1], bias_all[:], ALU.mult, ALU.add)
             nc.scalar.activation(mg[h][:], z[h][:], ACT.Sigmoid)
-        gather_b(0)
-        for h in range(2):
+        gather_b(2, b_raw[2])
+        turn_b(0, "b_raw0")
+        gather_b(SCALAR_TILE, b_cast, "z1")
+        turn_b(2)
+        spread_fade(0, "b_cast")
+        spread_fade(1, "b_picked2")
+        turn_b(SCALAR_TILE)
+        for h in range(I_TILES):
             nc.vector.scalar_tensor_tensor(slope[h][:], mg[h][:], 1.0, mg[h][:], ALU.subtract, ALU.mult)
             nc.vector.tensor_tensor(miss[h][:], mg[h][:], deg[:, h, :], ALU.subtract)
-        gather_b(1)
-        for h in range(2):
-            nc.vector.scalar_tensor_tensor(ds[h][:], miss[h][:], steep_col[h], slope[h][:], ALU.mult, ALU.mult)
-        g_in = sbuf("g_in", [P, I, 4], BF16)
-        g_in_pairs = g_in[:].rearrange("p i t -> p (i t)").bitcast(F32).rearrange("p (i u) -> p i u", u=2)
-        for h in range(2):
-            nc.vector.tensor_tensor(gs[h][:], w_ps[:], ds[h][:], ALU.mult)
-            pairs = gs[h][:].bitcast(F32)
+        for h in range(I_TILES):
+            nc.vector.scalar_tensor_tensor(ds[h][:], miss[h][:], steep_col[:, h : h + 1], slope[h][:], ALU.mult, ALU.mult)
+        g_grouped = [sbuf("g_grouped%d" % h, [P, P, PACK], BF16) for h in range(I_TILES)]
+        for h in range(I_TILES):
+            nc.vector.scalar_tensor_tensor(gs[h][:].rearrange("p (c r) -> p c r", r=PACK), w_ps[:].rearrange("p (r c) -> p c r", r=PACK),
+                                           -2.0, ds[h][:].rearrange("p (c r) -> p c r", r=PACK), ALU.mult, ALU.mult)
             turned = bank(3 + h)
-            for u in range(2):
-                nc.tensor.transpose(turned[:, P * u : P * (u + 1)], pairs[:, u : 2 * P : 2], ident[:])
-            nc.scalar.copy(g_in_pairs[:, P * h : P * (h + 1), :], turned[:, 0 : 2 * P].rearrange("p (u i) -> p i u", u=2))
-        quantize_b(0)
-        gather_b(2)
+            turn_pairs(gs[h][:], turned)
+            group_pairs(g_grouped[h][:], turned)
+        gather_b(3, b_raw[3], "ds0")
+        turn_b(3)
+        quantise_b(0, "gs0")
         g_codes = sbuf("g_codes", [P, I], U32)
         g_scales = sbuf("g_scales", [P, I], U8)
-        nc.vector.quantize_mx(out=g_codes[:].bitcast(FP8X4), scales=g_scales[:], in_=g_in[:].rearrange("p i t -> p (i t)"))
-        quantize_b(1)
-        gather_b(3)
+        for h in range(I_TILES):
+            quantise(block(g_codes, h), block(g_scales, h), g_grouped[h][:])
+        quantise_b(1, "gs1")
+        quantise_b(2, "ds1")
+        quantise_b(3)
 
-        gx = [sbuf("gx%d" % k, [P, I], F32) for k in range(4)]
-
-        def product(k):
-            gx_ps = bank((7, 2)[k % 2])
+        gx = [sbuf("gx%d" % k, [P, I], F32) for k in range(D_TILES)]
+        for k in range(D_TILES):
+            gx_ps = bank((7, 2, 0, 1)[k])
             nc.tensor.matmul_mx(out=gx_ps[:, 0:I], lhsT=bt_codes[k][:].bitcast(FP8X4), lhsT_scale=bt_scales[k][:],
                                 rhs=g_codes[:].bitcast(FP8X4), rhs_scale=g_scales[:], start=True, stop=True)
             nc.scalar.copy(gx[k][:], gx_ps[:, 0:I])
 
-        product(0)
-        product(1)
-        quantize_b(2)
-        quantize_b(3)
-        product(2)
-        product(3)
+        first = sbuf("faded_first", [P, BANK], F32, "slope1")
+        others = sbuf("faded_others", [P, POOL_TILES * T_HALVES - 1, BANK], F32, "bt_grouped3")
+        faded_rows = {}
+        for k in range(POOL_TILES):
+            for g in range(T_HALVES):
+                n = T_HALVES * k + g
+                faded_rows[k, g] = first[:] if n == 0 else others[:, n - 1, :]
+                nc.gpsimd.tensor_tensor(faded_rows[k, g], block(old_rows[k], g, BANK), fade_all[g][:], ALU.mult)
 
-        faded_t = [sbuf("faded_t%d" % c, [P, D], F32) for c in range(8)]
-        for c in range(8):
-            turned = bank(5 + c % 2)
-            for k in range(4):
-                nc.tensor.transpose(turned[:, P * k : P * (k + 1)], old_raw[c // 4][:, k, P * (c % 4) : P * (c % 4 + 1)], ident[:])
-            nc.scalar.activation(faded_t[c][:], turned[:], ACT.Copy, scale=late_cols[:, ROW_FADE + c : ROW_FADE + c + 1])
+        width = P * (D_TILES - POOL_TILES)
+        faded_t = [sbuf("faded_t%d" % c, [P, width], F32) for c in range(T_CHUNKS)]
+        for m in range(T_CHUNKS // 2):
+            turned = bank((7, 2, 0, 7)[m])
+            for e in range(2):
+                c = 2 * m + e
+                for k in range(D_TILES - POOL_TILES):
+                    nc.tensor.transpose(block(turned, 2 * e + k), block(old_half[c // 4][:, k, :], c % 4), ident[:])
+            for e in range(2):
+                c = 2 * m + e
+                nc.scalar.activation(faded_t[c][:], block(turned, e, width), ACT.Copy, scale=fade_col[:, c : c + 1])
 
-        back_banks = ((3, 4), (5, 6), (0, 1), (3, 4))
-        for k in range(4):
+        for k in range(D_TILES):
             nc.vector.tensor_copy(gf[k][:].indirect(list_i[:]), gx[k][:])
-            for g in range(2):
-                faded = bank(back_banks[k][g])
-                for c in range(4):
-                    nc.tensor.transpose(faded[:, P * c : P * (c + 1)], faded_t[4 * g + c][:, P * k : P * (k + 1)], ident[:])
+        for k in range(D_TILES):
+            for g in range(T_HALVES):
                 res = sbuf("res%d_%d" % (k, g), [P, BANK], F32)
-                nc.vector.tensor_tensor(res[:], faded[:], gf[k][:, BANK * g : BANK * (g + 1)], ALU.add)
-                nc.sync.dma_start(out[P * k : P * (k + 1), BANK * g : BANK * (g + 1)], res[:])
+                if k < POOL_TILES:
+                    nc.gpsimd.tensor_tensor(res[:], faded_rows[k, g], block(gf[k], g, BANK), ALU.add)
+                else:
+                    faded = bank(3 + T_HALVES * (k - POOL_TILES) + g)
+                    for c in range(BANK // P):
+                        nc.tensor.transpose(block(faded, c), block(faded_t[4 * g + c], k - POOL_TILES), ident[:])
+                    nc.vector.tensor_tensor(res[:], faded[:], block(gf[k], g, BANK), ALU.add)
+                queue = nc.scalar if k < POOL_TILES else nc.sync
+                queue.dma_start(block(rows_of(out, k), g, BANK), res[:])

@@ -25,7 +25,8 @@ I_TILES = I // P
 T_HALVES = T // BANK
 T_CHUNKS = T // P
 POOL_TILES = 2
-SCALAR_TILE = 1
+EARLY_TILES = 2
+SCALAR_TILE = 2
 
 
 def tile_attend_bpairfit_x_kernel(tc, taba, tabb_words, tabb_scales, steep, bias, degree, pw, js, brows, old, fade,
@@ -69,7 +70,8 @@ def tile_attend_bpairfit_x_kernel(tc, taba, tabb_words, tabb_scales, steep, bias
         fade_rows = sbuf("fade_rows", [P, P], F32)
         ident = sbuf("ident", [P, P], F32)
         warm = sbuf("warm", [P, 1], F32)
-        a_plane = [sbuf("a_plane%d" % t, [P, T], F32) for t in range(PACK)]
+        a_pair = sbuf("a_pair", [P, 2, T], F32)
+        a_plane = [a_pair[:, 0, :], a_pair[:, 1, :]] + [sbuf("a_plane%d" % t, [P, T], F32)[:] for t in (2, 3)]
         b_raw = [sbuf("b_raw%d" % k, [P, U], F32) for k in range(D_TILES)]
         old_rows = [sbuf("old_rows%d" % k, [P, T], F32) for k in range(POOL_TILES)]
         old_half = [sbuf("old_half%d" % g, [P, D_TILES - POOL_TILES, BANK], F32) for g in range(T_HALVES)]
@@ -85,36 +87,49 @@ def tile_attend_bpairfit_x_kernel(tc, taba, tabb_words, tabb_scales, steep, bias
         for k in range(D_TILES):
             (nc.vector, nc.gpsimd)[k // 2].memset(gf[k][:].bitcast(I32), 0)
 
-        def load_scales(q):
-            nc.sync.dma_start(scales[32 * q : 32 * q + 4, :].bitcast(I32), tabb_scales[0, 4 * q : 4 * q + 4, :].bitcast(I32))
-
         taba_planes = taba.rearrange("(p t) c -> p t c", t=PACK)
-        nc.sync.dma_start(list_i[:], offs)
-        nc.sync.dma_start(a_plane[0][:], taba_planes[:, 0, :])
         nc.sync.dma_start(list_j[:], offs2)
+        nc.sync.dma_start(list_i[:], offs)
         nc.sync.dma_start(words[:].bitcast(I32), tabb_words[0].bitcast(I32))
-        for q in range(3):
-            load_scales(q)
-        nc.sync.dma_start(a_plane[1][:], taba_planes[:, 1, :])
-        load_scales(3)
-        for t in (2, 3):
-            nc.sync.dma_start(a_plane[t][:], taba_planes[:, t, :])
+        for q in range(4):
+            nc.sync.dma_start(scales[32 * q : 32 * q + 4, :].bitcast(I32), tabb_scales[0, 4 * q : 4 * q + 4, :].bitcast(I32))
+        nc.sync.dma_start(a_pair[:], taba_planes[:, 0:2, :])
+        nc.sync.dma_start(a_plane[2], taba_planes[:, 2, :])
+        nc.sync.dma_start(fade_rows[0:T_CHUNKS, :], fade.rearrange("o (c p) -> (o c) p", p=P))
+        nc.sync.dma_start(a_plane[3], taba_planes[:, 3, :])
         nc.sync.dma_start(bias_col[:], bias.rearrange("o (p r) -> (o p) r", r=PACK))
         with nc.allow_non_contiguous_dma(reason="one steepness to a partition"):
             nc.sync.dma_start(steep_col[:], steep.rearrange("(h p) o -> p (h o)", p=P))
-        for k in (0, 1):
-            nc.sync.dma_start(b_raw[k][:], rows_of(brows, k))
+        nc.sync.dma_start(b_raw[0][:], rows_of(brows, 0))
+        nc.sync.dma_start(old_rows[0][:], rows_of(old, 0))
+        nc.sync.dma_start(b_raw[2][:], rows_of(brows, 2))
         nc.sync.dma_start(pw_col[:], pw.rearrange("o (p r) -> (o p) r", r=PACK))
         nc.sync.dma_start(js_col[:], js.rearrange("o (p r) -> (o p) r", r=PACK))
-        nc.sync.dma_start(fade_rows[0:T_CHUNKS, :], fade.rearrange("o (c p) -> (o c) p", p=P))
-        nc.sync.dma_start(b_raw[2][:], rows_of(brows, 2))
+        nc.sync.dma_start(b_raw[1][:], rows_of(brows, 1))
         nc.sync.dma_start(deg[:], degree.rearrange("(h p) j -> p h j", p=P))
         nc.sync.dma_start(b_raw[3][:], rows_of(brows, 3))
-        for k in range(POOL_TILES):
-            nc.sync.dma_start(old_rows[k][:], rows_of(old, k))
+        nc.sync.dma_start(old_rows[1][:], rows_of(old, 1))
         old_rest = old[P * POOL_TILES :, :].rearrange("(k p) t -> p k t", p=P)
         for g in range(T_HALVES):
             nc.sync.dma_start(old_half[g][:], old_rest[:, :, BANK * g : BANK * (g + 1)])
+
+        fade_ps = bank(7)
+        nc.tensor.transpose(block(fade_ps, 0), fade_rows[:], ident[:])
+        fade_col = sbuf("fade_col", [P, T_CHUNKS], F32)
+        nc.scalar.copy(fade_col[:], fade_ps[:, 0:T_CHUNKS])
+
+        fade_all = {}
+
+        def spread_fade(g):
+            spread_ps = bank(5 + g)
+            for c in range(BANK // P):
+                chunk = g * (BANK // P) + c
+                spread(spread_ps, fade_col[:, chunk : chunk + 1], c)
+            fade_all[g] = sbuf("fade_all%d" % g, [P, BANK], F32)
+            nc.scalar.copy(fade_all[g][:], spread_ps[:])
+
+        for g in range(T_HALVES):
+            spread_fade(g)
 
         bias_ps = bank(1)
         for r in range(PACK):
@@ -125,18 +140,21 @@ def tile_attend_bpairfit_x_kernel(tc, taba, tabb_words, tabb_scales, steep, bias
         a_picked = sbuf("a_picked", [P, PACK, I], F32)
         b_words = sbuf("b_words", [P, J], U16)
         b_scales = sbuf("b_scales", [P, J], U8)
-        nc.vector.tensor_copy(a_picked[:, 0, :], a_plane[0][:].indirect(list_i[:]))
         nc.vector.tensor_copy(b_words[:], words[:].indirect(list_j[:]))
         nc.vector.tensor_copy(b_scales[:], scales[:].indirect(list_j[:]))
-        for t in range(1, PACK):
-            nc.vector.tensor_copy(a_picked[:, t, :], a_plane[t][:].indirect(list_i[:]))
-        a_grouped = sbuf("a_grouped", [P, I, PACK], BF16)
-        nc.vector.tensor_copy(a_grouped[:].rearrange("p (c i) t -> p c t i", i=4), a_picked[:].rearrange("p t (c i) -> p c t i", i=4))
+        for t in range(PACK - 1):
+            nc.vector.tensor_copy(a_picked[:, t, :], a_plane[t].indirect(list_i[:]))
+        for h in range(I_TILES):
+            nc.vector.tensor_copy(block(a_picked[:, PACK - 1, :], h), a_plane[PACK - 1].indirect(block(list_i, h, P // 16)))
+        a_grouped = [sbuf("a_grouped%d" % h, [P, P, PACK], BF16) for h in range(I_TILES)]
+        for h in range(I_TILES):
+            nc.vector.tensor_copy(a_grouped[h][:].rearrange("p (c i) t -> p c t i", i=4),
+                                  a_picked[:, :, P * h : P * (h + 1)].rearrange("p t (c i) -> p c t i", i=4))
         a_codes = sbuf("a_codes", [P, I], U32)
         a_scales = sbuf("a_scales", [P, I], U8)
-        quantise(a_codes[:], a_scales[:], a_grouped[:])
         s_ps = [bank(3 + h) for h in range(I_TILES)]
         for h in range(I_TILES):
+            quantise(block(a_codes, h), block(a_scales, h), a_grouped[h][:])
             nc.tensor.matmul_mx(out=s_ps[h][:], lhsT=block(a_codes, h).bitcast(FP8X4), lhsT_scale=block(a_scales, h),
                                 rhs=b_words[:].bitcast(FP4X4), rhs_scale=b_scales[:], start=True, stop=True)
 
@@ -145,12 +163,8 @@ def tile_attend_bpairfit_x_kernel(tc, taba, tabb_words, tabb_scales, steep, bias
         w_ps = bank(2)
         for r in range(PACK):
             spread(w_ps, w_col[:, r : r + 1], r)
-        fade_ps = bank(7)
-        nc.tensor.transpose(block(fade_ps, 0), fade_rows[:], ident[:])
-        fade_col = sbuf("fade_col", [P, T_CHUNKS], F32)
-        nc.scalar.copy(fade_col[:], fade_ps[:, 0:T_CHUNKS])
 
-        b_picked, bt_grouped, bt_codes, bt_scales, fade_all = {}, {}, {}, {}, {}
+        b_picked, bt_grouped, bt_codes, bt_scales = {}, {}, {}, {}
 
         def gather_b(k, window, after=None):
             b_picked[k] = sbuf("b_picked%d" % k, [P, J], BF16, after)
@@ -170,69 +184,102 @@ def tile_attend_bpairfit_x_kernel(tc, taba, tabb_words, tabb_scales, steep, bias
             bt_scales[k] = sbuf("bt_scales%d" % k, [P, P], U8)
             quantise(bt_codes[k][:], bt_scales[k][:], bt_grouped[k][:])
 
-        def spread_fade(g, after):
-            spread_ps = bank(5 + g)
-            for c in range(BANK // P):
-                chunk = g * (BANK // P) + c
-                spread(spread_ps, fade_col[:, chunk : chunk + 1], c)
-            fade_all[g] = sbuf("fade_all%d" % g, [P, BANK], F32, after)
-            nc.scalar.copy(fade_all[g][:], spread_ps[:])
+        faded_rows = {}
 
+        def fade_rows_of(k, g, after=None):
+            faded_rows[k, g] = sbuf("faded_rows%d_%d" % (k, g), [P, BANK], F32, after)[:]
+            nc.gpsimd.tensor_tensor(faded_rows[k, g], block(old_rows[k], g, BANK), fade_all[g][:], ALU.mult)
+
+        for g in range(T_HALVES):
+            fade_rows_of(0, g, "a_grouped%d" % (1 - g))
         b_cast = sbuf("b_cast", [P, U], BF16)
         nc.scalar.activation(b_cast[:], b_raw[SCALAR_TILE][:], ACT.Copy)
         gather_b(0, b_raw[0], "a_picked")
 
-        z = [sbuf("z0", [P, J], F32, "b_raw0"), sbuf("z1", [P, J], F32)]
+        z = [sbuf("z%d" % h, [P, J], F32) for h in range(I_TILES)]
         mg, slope, miss, ds = [[sbuf("%s%d" % (name, h), [P, J], F32) for h in range(I_TILES)] for name in ("mg", "slope", "miss", "ds")]
         gs = [sbuf("gs%d" % h, [P, J], BF16) for h in range(I_TILES)]
         for h in range(I_TILES):
             nc.vector.scalar_tensor_tensor(z[h][:], s_ps[h][:], steep_col[:, h : h + 1], bias_all[:], ALU.mult, ALU.add)
             nc.scalar.activation(mg[h][:], z[h][:], ACT.Sigmoid)
-        gather_b(2, b_raw[2])
-        turn_b(0, "b_raw0")
+        gather_b(1, b_raw[1])
+        turn_b(0, "z0")
         gather_b(SCALAR_TILE, b_cast, "z1")
-        turn_b(2)
-        spread_fade(0, "b_cast")
-        spread_fade(1, "b_picked2")
+        turn_b(1)
         turn_b(SCALAR_TILE)
-        for h in range(I_TILES):
-            nc.vector.scalar_tensor_tensor(slope[h][:], mg[h][:], 1.0, mg[h][:], ALU.subtract, ALU.mult)
-            nc.vector.tensor_tensor(miss[h][:], mg[h][:], deg[:, h, :], ALU.subtract)
-        for h in range(I_TILES):
-            nc.vector.scalar_tensor_tensor(ds[h][:], miss[h][:], steep_col[:, h : h + 1], slope[h][:], ALU.mult, ALU.mult)
         g_grouped = [sbuf("g_grouped%d" % h, [P, P, PACK], BF16) for h in range(I_TILES)]
-        for h in range(I_TILES):
+        g_codes = sbuf("g_codes", [P, I], U32)
+        g_scales = sbuf("g_scales", [P, I], U8)
+
+        def slope_of(h):
+            nc.vector.scalar_tensor_tensor(slope[h][:], mg[h][:], 1.0, mg[h][:], ALU.subtract, ALU.mult)
+
+        def miss_of(h):
+            nc.vector.tensor_tensor(miss[h][:], mg[h][:], deg[:, h, :], ALU.subtract)
+
+        def ds_of(h):
+            nc.vector.scalar_tensor_tensor(ds[h][:], miss[h][:], steep_col[:, h : h + 1], slope[h][:], ALU.mult, ALU.mult)
+
+        def gs_of(h):
             nc.vector.scalar_tensor_tensor(gs[h][:].rearrange("p (c r) -> p c r", r=PACK), w_ps[:].rearrange("p (r c) -> p c r", r=PACK),
                                            -2.0, ds[h][:].rearrange("p (c r) -> p c r", r=PACK), ALU.mult, ALU.mult)
             turned = bank(3 + h)
             turn_pairs(gs[h][:], turned)
             group_pairs(g_grouped[h][:], turned)
-        gather_b(3, b_raw[3], "ds0")
+
+        def product(target, k, columns):
+            nc.tensor.matmul_mx(out=target, lhsT=bt_codes[k][:].bitcast(FP8X4), lhsT_scale=bt_scales[k][:],
+                                rhs=g_codes[:, columns].bitcast(FP8X4), rhs_scale=g_scales[:, columns], start=True, stop=True)
+
+        gx_half = {}
+
+        def early_products(h, n):
+            gx_ps = bank(n)
+            for k in range(EARLY_TILES):
+                product(block(gx_ps, k), k, slice(P * h, P * (h + 1)))
+            for k in range(EARLY_TILES):
+                gx_half[k, h] = sbuf("gx_half%d_%d" % (k, h), [P, P], F32)
+                nc.scalar.copy(gx_half[k, h][:], block(gx_ps, k))
+
+        def scatter_half(k, h):
+            nc.vector.tensor_copy(gf[k][:].indirect(block(list_i, h, P // 16)), gx_half[k, h][:])
+
+        def late_product(k):
+            gx_ps = bank(k % 2)
+            product(gx_ps[:, 0:I], k, slice(0, I))
+            gx = sbuf("gx%d" % k, [P, I], F32)
+            nc.scalar.copy(gx[:], gx_ps[:, 0:I])
+            return gx
+
+        slope_of(0)
+        miss_of(0)
+        slope_of(1)
+        ds_of(0)
+        miss_of(1)
+        gs_of(0)
+        ds_of(1)
+        gs_of(1)
+        quantise_b(0, "ds0")
+        quantise_b(1, "miss1")
+        quantise_b(2, "slope1")
+        quantise(block(g_codes, 0), block(g_scales, 0), g_grouped[0][:])
+        early_products(0, 7)
+        gather_b(3, b_raw[3], "bt_grouped2")
         turn_b(3)
-        quantise_b(0, "gs0")
-        g_codes = sbuf("g_codes", [P, I], U32)
-        g_scales = sbuf("g_scales", [P, I], U8)
-        for h in range(I_TILES):
-            quantise(block(g_codes, h), block(g_scales, h), g_grouped[h][:])
-        quantise_b(1, "gs1")
-        quantise_b(2, "ds1")
+        quantise(block(g_codes, 1), block(g_scales, 1), g_grouped[1][:])
+        early_products(1, 2)
+        gx_late = {2: late_product(2)}
+        for k in range(EARLY_TILES):
+            scatter_half(k, 0)
         quantise_b(3)
+        gx_late[3] = late_product(3)
+        for k in range(EARLY_TILES):
+            scatter_half(k, 1)
+        for k in range(EARLY_TILES, D_TILES):
+            nc.vector.tensor_copy(gf[k][:].indirect(list_i[:]), gx_late[k][:])
 
-        gx = [sbuf("gx%d" % k, [P, I], F32) for k in range(D_TILES)]
-        for k in range(D_TILES):
-            gx_ps = bank((7, 2, 0, 1)[k])
-            nc.tensor.matmul_mx(out=gx_ps[:, 0:I], lhsT=bt_codes[k][:].bitcast(FP8X4), lhsT_scale=bt_scales[k][:],
-                                rhs=g_codes[:].bitcast(FP8X4), rhs_scale=g_scales[:], start=True, stop=True)
-            nc.scalar.copy(gx[k][:], gx_ps[:, 0:I])
-
-        first = sbuf("faded_first", [P, BANK], F32, "slope1")
-        others = sbuf("faded_others", [P, POOL_TILES * T_HALVES - 1, BANK], F32, "bt_grouped3")
-        faded_rows = {}
-        for k in range(POOL_TILES):
-            for g in range(T_HALVES):
-                n = T_HALVES * k + g
-                faded_rows[k, g] = first[:] if n == 0 else others[:, n - 1, :]
-                nc.gpsimd.tensor_tensor(faded_rows[k, g], block(old_rows[k], g, BANK), fade_all[g][:], ALU.mult)
+        for g in range(T_HALVES):
+            fade_rows_of(1, g, "g_grouped%d" % g)
 
         width = P * (D_TILES - POOL_TILES)
         faded_t = [sbuf("faded_t%d" % c, [P, width], F32) for c in range(T_CHUNKS)]
@@ -246,11 +293,10 @@ def tile_attend_bpairfit_x_kernel(tc, taba, tabb_words, tabb_scales, steep, bias
                 c = 2 * m + e
                 nc.scalar.activation(faded_t[c][:], block(turned, e, width), ACT.Copy, scale=fade_col[:, c : c + 1])
 
-        for k in range(D_TILES):
-            nc.vector.tensor_copy(gf[k][:].indirect(list_i[:]), gx[k][:])
+        res_left = sbuf("res_left", [P, D_TILES - POOL_TILES, BANK], F32, "old_half1")
         for k in range(D_TILES):
             for g in range(T_HALVES):
-                res = sbuf("res%d_%d" % (k, g), [P, BANK], F32)
+                res = res_left[:, k - POOL_TILES, :] if k >= POOL_TILES and g == 0 else sbuf("res%d_%d" % (k, g), [P, BANK], F32)
                 if k < POOL_TILES:
                     nc.gpsimd.tensor_tensor(res[:], faded_rows[k, g], block(gf[k], g, BANK), ALU.add)
                 else:
@@ -258,5 +304,5 @@ def tile_attend_bpairfit_x_kernel(tc, taba, tabb_words, tabb_scales, steep, bias
                     for c in range(BANK // P):
                         nc.tensor.transpose(block(faded, c), block(faded_t[4 * g + c], k - POOL_TILES), ident[:])
                     nc.vector.tensor_tensor(res[:], faded[:], block(gf[k], g, BANK), ALU.add)
-                queue = nc.scalar if k < POOL_TILES else nc.sync
+                queue = nc.sync if k < POOL_TILES else nc.scalar
                 queue.dma_start(block(rows_of(out, k), g, BANK), res[:])

@@ -101,14 +101,14 @@ def tile_attend_bpairfit_x_kernel(tc, taba, tabb_words, tabb_scales, steep, bias
         with nc.allow_non_contiguous_dma(reason="one steepness to a partition"):
             nc.sync.dma_start(steep_col[:], steep.rearrange("(h p) o -> p (h o)", p=P))
         nc.sync.dma_start(b_raw[0][:], rows_of(brows, 0))
-        nc.sync.dma_start(old_rows[0][:], rows_of(old, 0))
         nc.sync.dma_start(b_raw[2][:], rows_of(brows, 2))
         nc.sync.dma_start(pw_col[:], pw.rearrange("o (p r) -> (o p) r", r=PACK))
         nc.sync.dma_start(js_col[:], js.rearrange("o (p r) -> (o p) r", r=PACK))
         nc.sync.dma_start(b_raw[1][:], rows_of(brows, 1))
         nc.sync.dma_start(deg[:], degree.rearrange("(h p) j -> p h j", p=P))
         nc.sync.dma_start(b_raw[3][:], rows_of(brows, 3))
-        nc.sync.dma_start(old_rows[1][:], rows_of(old, 1))
+        for k in range(POOL_TILES):
+            nc.sync.dma_start(old_rows[k][:], rows_of(old, k))
         old_rest = old[P * POOL_TILES :, :].rearrange("(k p) t -> p k t", p=P)
         for g in range(T_HALVES):
             nc.sync.dma_start(old_half[g][:], old_rest[:, :, BANK * g : BANK * (g + 1)])
@@ -186,12 +186,10 @@ def tile_attend_bpairfit_x_kernel(tc, taba, tabb_words, tabb_scales, steep, bias
 
         faded_rows = {}
 
-        def fade_rows_of(k, g, after=None):
-            faded_rows[k, g] = sbuf("faded_rows%d_%d" % (k, g), [P, BANK], F32, after)[:]
+        def fade_rows_of(k, g, target):
+            faded_rows[k, g] = target
             nc.gpsimd.tensor_tensor(faded_rows[k, g], block(old_rows[k], g, BANK), fade_all[g][:], ALU.mult)
 
-        for g in range(T_HALVES):
-            fade_rows_of(0, g, "a_grouped%d" % (1 - g))
         b_cast = sbuf("b_cast", [P, U], BF16)
         nc.scalar.activation(b_cast[:], b_raw[SCALAR_TILE][:], ACT.Copy)
         gather_b(0, b_raw[0], "a_picked")
@@ -279,7 +277,8 @@ def tile_attend_bpairfit_x_kernel(tc, taba, tabb_words, tabb_scales, steep, bias
             nc.vector.tensor_copy(gf[k][:].indirect(list_i[:]), gx_late[k][:])
 
         for g in range(T_HALVES):
-            fade_rows_of(1, g, "g_grouped%d" % g)
+            fade_rows_of(0, g, sbuf("faded_rows0_%d" % g, [P, BANK], F32, "g_grouped%d" % g)[:])
+        second = sbuf("faded_rows1", [P, T], F32, "bt_grouped3")
 
         width = P * (D_TILES - POOL_TILES)
         faded_t = [sbuf("faded_t%d" % c, [P, width], F32) for c in range(T_CHUNKS)]
@@ -297,6 +296,8 @@ def tile_attend_bpairfit_x_kernel(tc, taba, tabb_words, tabb_scales, steep, bias
         for k in range(D_TILES):
             for g in range(T_HALVES):
                 res = res_left[:, k - POOL_TILES, :] if k >= POOL_TILES and g == 0 else sbuf("res%d_%d" % (k, g), [P, BANK], F32)
+                if k == 1:
+                    fade_rows_of(k, g, block(second, g, BANK))
                 if k < POOL_TILES:
                     nc.gpsimd.tensor_tensor(res[:], faded_rows[k, g], block(gf[k], g, BANK), ALU.add)
                 else:

from contextlib import ExitStack

import concourse.mybir as mybir
from concourse.masks import make_identity

D, T, U, I, J = 512, 1024, 1024, 256, 512
FLOPS = 2 * (2 * D * I * J)

F32 = mybir.dt.float32
BF16 = mybir.dt.bfloat16
I32 = mybir.dt.int32
U32 = mybir.dt.uint32
U16 = mybir.dt.uint16
U8 = mybir.dt.uint8
FP8X4 = mybir.dt.float8_e4m3fn_x4
FP4X4 = mybir.dt.float4_e2m1fn_x4
ALU = mybir.AluOpType
ACT = mybir.ActivationFunctionType

P = 128
PACK = 4
BANK = 512
D_TILES = D // P
I_TILES = I // P
T_HALVES = T // BANK
T_CHUNKS = T // P
POOL_TILES = 2
EARLY_TILES = 2
SCALAR_TILE = 2


def tile_attend_bpairfit_x_kernel(tc, taba, tabb_words, tabb_scales, steep, bias, degree, pw, js, brows, old, fade,
                                   offs, offs2, out):
    nc = tc.nc
    with ExitStack() as ctx:
        sb = ctx.enter_context(tc.tile_pool(name="sb", bufs=1))
        ps = ctx.enter_context(tc.psum_pool(name="ps", bufs=1))

        def bank(n):
            return ps.tile([P, BANK], F32, name="bank%d" % n, tag="bank%d" % n)

        def sbuf(name, shape, dtype, after=None):
            return sb.tile(shape, dtype, name=name, tag=after or name, align_bytes=64)

        def rows_of(x, k):
            return x[P * k : P * (k + 1), :]

        def block(x, c, width=P):
            return x[:, width * c : width * (c + 1)]

        def quantise(codes, scale_bytes, grouped):
            nc.vector.quantize_mx(out=codes.bitcast(FP8X4), scales=scale_bytes, in_=grouped.rearrange("p c t -> p (c t)"))

        def spread(target, column, c):
            nc.tensor.transpose(block(target, c), column.to_broadcast([P, P]), ident[:])

        def turn_pairs(values, target):
            pairs = values.bitcast(F32)
            for u in range(2):
                nc.tensor.transpose(block(target, u), pairs[:, u : 2 * P : 2], ident[:])

        def group_pairs(grouped, turned):
            nc.scalar.copy(grouped.rearrange("p c t -> p (c t)").bitcast(F32).rearrange("p (c u) -> p c u", u=2),
                           turned[:, 0 : 2 * P].rearrange("p (u c) -> p c u", u=2))

        list_i = sb.tile([P, I // 16], U16, name="list_i")
        list_j = sb.tile([P, J // 16], U16, name="list_j")
        words = sbuf("words", [P, U], U16)
        scales = sbuf("scales", [P, U], U8)
        fade_rows = sbuf("fade_rows", [P, P], F32)
        ident = sbuf("ident", [P, P], F32)
        warm = sbuf("warm", [P, 1], F32)
        a_pair = sbuf("a_pair", [P, 2, T], F32)
        a_plane = [a_pair[:, 0, :], a_pair[:, 1, :]] + [sbuf("a_plane%d" % t, [P, T], F32)[:] for t in (2, 3)]
        b_raw = [sbuf("b_raw%d" % k, [P, U], F32) for k in range(D_TILES)]
        old_rows = [sbuf("old_rows%d" % k, [P, T], F32) for k in range(POOL_TILES)]
        old_half = [sbuf("old_half%d" % g, [P, D_TILES - POOL_TILES, BANK], F32) for g in range(T_HALVES)]
        deg = sbuf("deg", [P, I_TILES, J], F32)
        bias_col, pw_col, js_col = [sbuf(name, [P, PACK], F32) for name in ("bias_col", "pw_col", "js_col")]
        steep_col = sbuf("steep_col", [P, I_TILES], F32)
        gf = [sbuf("gf%d" % k, [P, T], F32) for k in range(D_TILES)]

        nc.gpsimd.memset(scales[:].bitcast(I32), 0)
        nc.gpsimd.memset(fade_rows[:], 0.0)
        make_identity(nc, ident[:])
        nc.scalar.activation(warm[:], ident[:, 0:1], ACT.Sigmoid)
        for k in range(D_TILES):
            (nc.vector, nc.gpsimd)[k // 2].memset(gf[k][:].bitcast(I32), 0)

        taba_planes = taba.rearrange("(p t) c -> p t c", t=PACK)
        nc.sync.dma_start(list_j[:], offs2)
        nc.sync.dma_start(list_i[:], offs)
        nc.sync.dma_start(words[:].bitcast(I32), tabb_words[0].bitcast(I32))
        for q in range(4):
            nc.sync.dma_start(scales[32 * q : 32 * q + 4, :].bitcast(I32), tabb_scales[0, 4 * q : 4 * q + 4, :].bitcast(I32))
        nc.sync.dma_start(a_pair[:], taba_planes[:, 0:2, :])
        nc.sync.dma_start(a_plane[2], taba_planes[:, 2, :])
        nc.sync.dma_start(fade_rows[0:T_CHUNKS, :], fade.rearrange("o (c p) -> (o c) p", p=P))
        nc.sync.dma_start(a_plane[3], taba_planes[:, 3, :])
        nc.sync.dma_start(bias_col[:], bias.rearrange("o (p r) -> (o p) r", r=PACK))
        with nc.allow_non_contiguous_dma(reason="one steepness to a partition"):
            nc.sync.dma_start(steep_col[:], steep.rearrange("(h p) o -> p (h o)", p=P))
        nc.sync.dma_start(b_raw[0][:], rows_of(brows, 0))
        nc.sync.dma_start(b_raw[2][:], rows_of(brows, 2))
        nc.sync.dma_start(pw_col[:], pw.rearrange("o (p r) -> (o p) r", r=PACK))
        nc.sync.dma_start(js_col[:], js.rearrange("o (p r) -> (o p) r", r=PACK))
        nc.sync.dma_start(b_raw[1][:], rows_of(brows, 1))
        nc.sync.dma_start(deg[:], degree.rearrange("(h p) j -> p h j", p=P))
        nc.sync.dma_start(b_raw[3][:], rows_of(brows, 3))
        for k in range(POOL_TILES):
            nc.sync.dma_start(old_rows[k][:], rows_of(old, k))
        old_rest = old[P * POOL_TILES :, :].rearrange("(k p) t -> p k t", p=P)
        for g in range(T_HALVES):
            nc.sync.dma_start(old_half[g][:], old_rest[:, :, BANK * g : BANK * (g + 1)])

        fade_ps = bank(7)
        nc.tensor.transpose(block(fade_ps, 0), fade_rows[:], ident[:])
        fade_col = sbuf("fade_col", [P, T_CHUNKS], F32)
        nc.scalar.copy(fade_col[:], fade_ps[:, 0:T_CHUNKS])

        fade_all = {}

        def spread_fade(g):
            spread_ps = bank(5 + g)
            for c in range(BANK // P):
                chunk = g * (BANK // P) + c
                spread(spread_ps, fade_col[:, chunk : chunk + 1], c)
            fade_all[g] = sbuf("fade_all%d" % g, [P, BANK], F32)
            nc.scalar.copy(fade_all[g][:], spread_ps[:])

        for g in range(T_HALVES):
            spread_fade(g)

        bias_ps = bank(1)
        for r in range(PACK):
            spread(bias_ps, bias_col[:, r : r + 1], r)
        bias_all = sbuf("bias_all", [P, J], F32)
        nc.scalar.copy(bias_all[:].rearrange("p (c r) -> p c r", r=PACK), bias_ps[:].rearrange("p (r c) -> p c r", r=PACK))

        a_picked = sbuf("a_picked", [P, PACK, I], F32)
        b_words = sbuf("b_words", [P, J], U16)
        b_scales = sbuf("b_scales", [P, J], U8)
        nc.vector.tensor_copy(b_words[:], words[:].indirect(list_j[:]))
        nc.vector.tensor_copy(b_scales[:], scales[:].indirect(list_j[:]))
        for t in range(PACK - 1):
            nc.vector.tensor_copy(a_picked[:, t, :], a_plane[t].indirect(list_i[:]))
        for h in range(I_TILES):
            nc.vector.tensor_copy(block(a_picked[:, PACK - 1, :], h), a_plane[PACK - 1].indirect(block(list_i, h, P // 16)))
        a_grouped = [sbuf("a_grouped%d" % h, [P, P, PACK], BF16) for h in range(I_TILES)]
        for h in range(I_TILES):
            nc.vector.tensor_copy(a_grouped[h][:].rearrange("p (c i) t -> p c t i", i=4),
                                  a_picked[:, :, P * h : P * (h + 1)].rearrange("p t (c i) -> p c t i", i=4))
        a_codes = sbuf("a_codes", [P, I], U32)
        a_scales = sbuf("a_scales", [P, I], U8)
        s_ps = [bank(3 + h) for h in range(I_TILES)]
        for h in range(I_TILES):
            quantise(block(a_codes, h), block(a_scales, h), a_grouped[h][:])
            nc.tensor.matmul_mx(out=s_ps[h][:], lhsT=block(a_codes, h).bitcast(FP8X4), lhsT_scale=block(a_scales, h),
                                rhs=b_words[:].bitcast(FP4X4), rhs_scale=b_scales[:], start=True, stop=True)

        w_col = sbuf("w_col", [P, PACK], F32)
        nc.gpsimd.tensor_tensor(w_col[:], pw_col[:], js_col[:], ALU.mult)
        w_ps = bank(2)
        for r in range(PACK):
            spread(w_ps, w_col[:, r : r + 1], r)

        b_picked, bt_grouped, bt_codes, bt_scales = {}, {}, {}, {}

        def gather_b(k, window, after=None):
            b_picked[k] = sbuf("b_picked%d" % k, [P, J], BF16, after)
            if k == SCALAR_TILE:
                nc.scalar.activation(b_picked[k][:], window[:].indirect(list_j[:]), ACT.Copy)
            else:
                nc.vector.tensor_copy(b_picked[k][:], window[:].indirect(list_j[:]))

        def turn_b(k, after=None):
            turned = bank(k % 2)
            turn_pairs(b_picked[k][:], turned)
            bt_grouped[k] = sbuf("bt_grouped%d" % k, [P, P, PACK], BF16, after)
            group_pairs(bt_grouped[k][:], turned)

        def quantise_b(k, after=None):
            bt_codes[k] = sbuf("bt_codes%d" % k, [P, P], U32, after)
            bt_scales[k] = sbuf("bt_scales%d" % k, [P, P], U8)
            quantise(bt_codes[k][:], bt_scales[k][:], bt_grouped[k][:])

        faded_rows = {}

        def fade_rows_of(k, g, target):
            faded_rows[k, g] = target
            nc.gpsimd.tensor_tensor(faded_rows[k, g], block(old_rows[k], g, BANK), fade_all[g][:], ALU.mult)

        b_cast = sbuf("b_cast", [P, U], BF16)
        nc.scalar.activation(b_cast[:], b_raw[SCALAR_TILE][:], ACT.Copy)
        gather_b(0, b_raw[0], "a_picked")

        z = [sbuf("z%d" % h, [P, J], F32) for h in range(I_TILES)]
        mg, slope, miss, ds = [[sbuf("%s%d" % (name, h), [P, J], F32) for h in range(I_TILES)] for name in ("mg", "slope", "miss", "ds")]
        gs = [sbuf("gs%d" % h, [P, J], BF16) for h in range(I_TILES)]
        for h in range(I_TILES):
            nc.vector.scalar_tensor_tensor(z[h][:], s_ps[h][:], steep_col[:, h : h + 1], bias_all[:], ALU.mult, ALU.add)
            nc.scalar.activation(mg[h][:], z[h][:], ACT.Sigmoid)
        gather_b(1, b_raw[1])
        turn_b(0, "z0")
        gather_b(SCALAR_TILE, b_cast, "z1")
        turn_b(1)
        turn_b(SCALAR_TILE)
        g_grouped = [sbuf("g_grouped%d" % h, [P, P, PACK], BF16) for h in range(I_TILES)]
        g_codes = sbuf("g_codes", [P, I], U32)
        g_scales = sbuf("g_scales", [P, I], U8)

        def slope_of(h):
            nc.vector.scalar_tensor_tensor(slope[h][:], mg[h][:], 1.0, mg[h][:], ALU.subtract, ALU.mult)

        def miss_of(h):
            nc.vector.tensor_tensor(miss[h][:], mg[h][:], deg[:, h, :], ALU.subtract)

        def ds_of(h):
            nc.vector.scalar_tensor_tensor(ds[h][:], miss[h][:], steep_col[:, h : h + 1], slope[h][:], ALU.mult, ALU.mult)

        def gs_of(h):
            nc.vector.scalar_tensor_tensor(gs[h][:].rearrange("p (c r) -> p c r", r=PACK), w_ps[:].rearrange("p (r c) -> p c r", r=PACK),
                                           -2.0, ds[h][:].rearrange("p (c r) -> p c r", r=PACK), ALU.mult, ALU.mult)
            turned = bank(3 + h)
            turn_pairs(gs[h][:], turned)
            group_pairs(g_grouped[h][:], turned)

        def product(target, k, columns):
            nc.tensor.matmul_mx(out=target, lhsT=bt_codes[k][:].bitcast(FP8X4), lhsT_scale=bt_scales[k][:],
                                rhs=g_codes[:, columns].bitcast(FP8X4), rhs_scale=g_scales[:, columns], start=True, stop=True)

        gx_half = {}

        def early_products(h, n):
            gx_ps = bank(n)
            for k in range(EARLY_TILES):
                product(block(gx_ps, k), k, slice(P * h, P * (h + 1)))
            for k in range(EARLY_TILES):
                gx_half[k, h] = sbuf("gx_half%d_%d" % (k, h), [P, P], F32)
                nc.scalar.copy(gx_half[k, h][:], block(gx_ps, k))

        def scatter_half(k, h):
            nc.vector.tensor_copy(gf[k][:].indirect(block(list_i, h, P // 16)), gx_half[k, h][:])

        def late_product(k):
            gx_ps = bank(k % 2)
            product(gx_ps[:, 0:I], k, slice(0, I))
            gx = sbuf("gx%d" % k, [P, I], F32)
            nc.scalar.copy(gx[:], gx_ps[:, 0:I])
            return gx

        slope_of(0)
        miss_of(0)
        slope_of(1)
        ds_of(0)
        miss_of(1)
        gs_of(0)
        ds_of(1)
        gs_of(1)
        quantise_b(0, "ds0")
        quantise_b(1, "miss1")
        quantise_b(2, "slope1")
        quantise(block(g_codes, 0), block(g_scales, 0), g_grouped[0][:])
        early_products(0, 7)
        gather_b(3, b_raw[3], "bt_grouped2")
        turn_b(3)
        quantise(block(g_codes, 1), block(g_scales, 1), g_grouped[1][:])
        early_products(1, 2)
        gx_late = {2: late_product(2)}
        for k in range(EARLY_TILES):
            scatter_half(k, 0)
        quantise_b(3)
        gx_late[3] = late_product(3)
        for k in range(EARLY_TILES):
            scatter_half(k, 1)
        for k in range(EARLY_TILES, D_TILES):
            nc.vector.tensor_copy(gf[k][:].indirect(list_i[:]), gx_late[k][:])

        for g in range(T_HALVES):
            fade_rows_of(0, g, sbuf("faded_rows0_%d" % g, [P, BANK], F32, "g_grouped%d" % g)[:])
        second = sbuf("faded_rows1", [P, T], F32, "bt_grouped3")

        width = P * (D_TILES - POOL_TILES)
        faded_t = [sbuf("faded_t%d" % c, [P, width], F32) for c in range(T_CHUNKS)]
        for m in range(T_CHUNKS // 2):
            turned = bank((7, 2, 0, 7)[m])
            for e in range(2):
                c = 2 * m + e
                for k in range(D_TILES - POOL_TILES):
                    nc.tensor.transpose(block(turned, 2 * e + k), block(old_half[c // 4][:, k, :], c % 4), ident[:])
            for e in range(2):
                c = 2 * m + e
                nc.scalar.activation(faded_t[c][:], block(turned, e, width), ACT.Copy, scale=fade_col[:, c : c + 1])

        res_left = sbuf("res_left", [P, D_TILES - POOL_TILES, BANK], F32, "old_half1")
        for k in range(D_TILES):
            for g in range(T_HALVES):
                res = res_left[:, k - POOL_TILES, :] if k >= POOL_TILES and g == 0 else sbuf("res%d_%d" % (k, g), [P, BANK], F32)
                if k == 1:
                    fade_rows_of(k, g, block(second, g, BANK))
                if k < POOL_TILES:
                    nc.gpsimd.tensor_tensor(res[:], faded_rows[k, g], block(gf[k], g, BANK), ALU.add)
                else:
                    faded = bank(3 + T_HALVES * (k - POOL_TILES) + g)
                    for c in range(BANK // P):
                        nc.tensor.transpose(block(faded, c), block(faded_t[4 * g + c], k - POOL_TILES), ident[:])
                    nc.vector.tensor_tensor(res[:], faded[:], block(gf[k], g, BANK), ALU.add)
                queue = nc.sync if k < POOL_TILES else nc.scalar
                queue.dma_start(block(rows_of(out, k), g, BANK), res[:])
